import numpy as np
import ml_dtypes


def mxq(x, axis, fmt="e4m3"):
    dtype, down = {"e4m3": (ml_dtypes.float8_e4m3fn, 7), "e5m2": (ml_dtypes.float8_e5m2, 14)}[fmt]
    v = np.moveaxis(np.asarray(x, np.float32).astype(ml_dtypes.bfloat16).astype(np.float64), axis, -1)
    blocks = v.reshape(v.shape[:-1] + (-1, 32))
    amax = np.abs(blocks).max(-1, keepdims=True)
    byte = np.maximum(np.where(amax > 0, np.frexp(amax)[1] - 1 + 127, 0) - down, 1)
    scale = np.exp2(byte - 127.0)
    codes = (blocks / scale).astype(np.float32).astype(dtype).astype(np.float64)
    return np.moveaxis((codes * scale).reshape(v.shape), -1, axis)


WIDE = False


def mx_kscale(k):
    if not WIDE:
        return np.ones(k)
    levels = np.array([10, -10, 5, -5, 0])
    if k % 512:
        return np.exp2(np.random.permutation(np.resize(levels, k // 32))).repeat(32)
    a = np.empty((k // 512, 16))
    for p in range(k // 512):
        a[p, :8] = np.random.permutation(np.resize(levels, 8))
        for g in range(8):
            far = levels[np.abs(levels - a[p, g]) >= 10]
            a[p, g + 8] = far[np.random.randint(len(far))]
    return np.exp2(a.ravel()).repeat(32)


def f64(x):
    return np.asarray(x).astype(np.float64)


def striped8(idx):
    return np.asarray(idx).reshape(8, -1, 16).transpose(0, 2, 1).reshape(128, -1).astype(np.uint16)


def unstriped8(offs):
    return offs.reshape(8, 16, -1).transpose(0, 2, 1).reshape(8, -1).astype(np.int64)


def pick8(x, idx, run):
    r = np.arange(len(x))
    return x[r[:, None], idx[r % (8 * run) // run]]


E2M1 = np.array([0.0, 0.5, 1.0, 1.5, 2.0, 3.0, 4.0, 6.0, -0.0, -0.5, -1.0, -1.5, -2.0, -3.0, -4.0, -6.0])


def pack_weight(w, fmt):
    k, n = w.shape
    w = f64(np.asarray(w, np.float32).astype(ml_dtypes.bfloat16)).reshape(k // 32, 32, n)
    amax = np.abs(w).max(1)
    if fmt == "e4m3":
        byte = np.frexp(amax)[1] - 1 + 127 - 7
    else:
        mant, ex = np.frexp(amax / 6.0)
        byte = np.where(mant > 0.5, ex, ex - 1) + 127
    byte = np.clip(np.where(amax > 0, byte, 1), 1, 254)
    scaled = (w * np.exp2(127.0 - byte)[:, None, :]).reshape(k, n).astype(np.float32)
    by_word = np.ascontiguousarray(scaled.reshape(k // 512, 128, 4, n).transpose(0, 1, 3, 2))
    if fmt == "e4m3":
        words = by_word.astype(ml_dtypes.float8_e4m3fn).view(np.uint8)
    else:
        c = by_word.astype(ml_dtypes.float4_e2m1fn).view(np.uint8) & 0xF
        words = (c[..., 0::2] | (c[..., 1::2] << 4)).reshape(k // 512, 128, 2 * n)
    return np.ascontiguousarray(words), np.ascontiguousarray(byte.astype(np.uint8).reshape(k // 512, 16, n))


def unpack_weight(words, scales, fmt):
    g, _, n = scales.shape
    words = np.ascontiguousarray(words).reshape(g, 128, n, -1)
    if fmt == "e4m3":
        vals = words.view(ml_dtypes.float8_e4m3fn).astype(np.float64)
    else:
        nib = np.empty((g, 128, n, 4), np.uint8)
        nib[..., 0::2] = words & 0xF
        nib[..., 1::2] = words >> 4
        vals = E2M1[nib]
    vals = vals * np.repeat(np.exp2(scales.astype(np.float64) - 127.0), 8, axis=1)[..., None]
    return vals.transpose(0, 1, 3, 2).reshape(g * 512, n)


D, T, U, Z, I, Q = 512, 1024, 1024, 1024, 512, 128


def setup_inputs():
    n = np.random.standard_normal
    idx = np.stack([np.random.permutation(T)[:I] for _ in range(8)])
    idx2 = np.stack([np.random.permutation(U)[:I] for _ in range(8)])
    idx3 = np.stack([np.random.permutation(Z)[:I] for _ in range(8)])
    idx4 = np.stack([np.random.permutation(Z)[:I] for _ in range(8)])
    idx5 = np.stack([np.random.permutation(U)[:I] for _ in range(8)])
    idx6 = np.stack([np.random.permutation(T)[:I] for _ in range(8)])
    fd = mx_kscale(D)
    keysp = pack_weight(n((D, T)) / fd[:, None], "e4m3")
    notesp = pack_weight(n((D, U)) / fd[:, None], "e2m1")
    return {
        "query": (n((D, Q)) * 1.0 / np.sqrt(D) * fd[:, None]).astype(np.float32),
        "keys_words": keysp[0],
        "keys_scales": keysp[1],
        "notes_words": notesp[0],
        "notes_scales": notesp[1],
        "offs": striped8(idx),
        "offs2": striped8(idx2),
        "offs3": striped8(idx3),
        "offs4": striped8(idx4),
        "offs5": striped8(idx5),
        "offs6": striped8(idx6),
    }


def reference(query, keys_words, keys_scales, notes_words, notes_scales, offs, offs2, offs3, offs4, offs5, offs6):
    idx = unstriped8(offs)
    idx2 = unstriped8(offs2)
    idx3 = unstriped8(offs3)
    idx4 = unstriped8(offs4)
    idx5 = unstriped8(offs5)
    idx6 = unstriped8(offs6)
    keysu = unpack_weight(keys_words, keys_scales, "e4m3")
    notesu = unpack_weight(notes_words, notes_scales, "e2m1")
    queryq = mxq(f64(query), 0, "e4m3")
    a = queryq.T @ keysu
    b = queryq.T @ notesu
    f1 = np.zeros((Q, Z))
    f1[np.arange(Q)[:, None], idx3[np.arange(Q) % 128 // 16]] = pick8(a, idx, 16)
    f2 = np.zeros((Q, Z))
    f2[np.arange(Q)[:, None], idx4[np.arange(Q) % 128 // 16]] = pick8(b, idx2, 16)
    m1 = np.minimum(f1, f2)
    w = pick8(m1, idx3, 16) + pick8(m1, idx4, 16)
    v = w - pick8(b, idx5, 16)
    y = np.maximum(v, pick8(a, idx6, 16))
    return y

@@ -1,0 +1,147 @@
+from contextlib import ExitStack
+
+import concourse.mybir as mybir
+
+D, T, U, Z, I, Q = 512, 1024, 1024, 1024, 512, 128
+FLOPS = 2 * D * Q * (T + U)
+
+F32 = mybir.dt.float32
+BF16 = mybir.dt.bfloat16
+I32 = mybir.dt.int32
+U32 = mybir.dt.uint32
+U16 = mybir.dt.uint16
+U8 = mybir.dt.uint8
+FP8X4 = mybir.dt.float8_e4m3fn_x4
+FP4X4 = mybir.dt.float4_e2m1fn_x4
+ALU = mybir.AluOpType
+COPY = mybir.ActivationFunctionType.Copy
+
+P = 128
+PACK = 4
+HALF = I // 2
+LIST_COLS = I // 16
+
+
+def tile_attend_foldedback_two_kernel(
+    tc, query, keys_words, keys_scales, notes_words, notes_scales, offs, offs2, offs3, offs4, offs5, offs6, out
+):
+    nc = tc.nc
+    with ExitStack() as ctx:
+        lists = ctx.enter_context(tc.tile_pool(name="lists", bufs=1))
+        sb = ctx.enter_context(tc.tile_pool(name="sb", bufs=1))
+        psum = ctx.enter_context(tc.psum_pool(name="psum", bufs=1))
+
+        def load_list(src, name):
+            t = lists.tile([P, LIST_COLS], U16, name=name)
+            nc.sync.dma_start(t[:], src)
+            return t
+
+        def load_plane(queue, plane, scales):
+            for quad in range(4):
+                queue.dma_start(
+                    plane[32 * quad : 32 * quad + 4, :].bitcast(I32),
+                    scales[0, 4 * quad : 4 * quad + 4, :].bitcast(I32),
+                )
+
+        def half(t, h):
+            return t[:, h * (LIST_COLS // 2) : (h + 1) * (LIST_COLS // 2)]
+
+        notes_plane = sb.tile([P, U], U8, align_bytes=64)
+        keys_plane = sb.tile([P, T], U8, align_bytes=64)
+        nc.vector.memset(notes_plane[:].bitcast(I32), 0)
+        nc.vector.memset(keys_plane[:].bitcast(I32), 0)
+
+        q_raw = sb.tile([P, PACK, Q], F32)
+        nc.sync.dma_start(q_raw[:], query.rearrange("(p j) w -> p j w", j=PACK))
+        notes_codes = sb.tile([P, 2 * U], U8, align_bytes=64)
+        nc.sync.dma_start(notes_codes[:].bitcast(I32), notes_words[0].bitcast(I32))
+        load_plane(nc.sync, notes_plane, notes_scales)
+        list2 = load_list(offs2, "list2")
+        list4 = load_list(offs4, "list4")
+        keys_codes = sb.tile([P, T], U32, align_bytes=64)
+        nc.sync.dma_start(keys_codes[:].bitcast(I32), keys_words[0].rearrange("p n t -> p (n t)").bitcast(I32))
+        load_plane(nc.sync, keys_plane, keys_scales)
+        list1 = load_list(offs, "list1")
+        list3 = load_list(offs3, "list3")
+        list5 = load_list(offs5, "list5")
+        list6 = load_list(offs6, "list6")
+
+        f1 = sb.tile([P, Z], F32)
+        f2 = sb.tile([P, Z], F32)
+        nc.vector.memset(f2[:], 0.0)
+        nc.gpsimd.memset(f1[:], 0.0)
+
+        q_grouped = sb.tile([P, Q, PACK], BF16, align_bytes=64)
+        nc.vector.tensor_copy(q_grouped[:], q_raw[:].rearrange("p j w -> p w j"))
+        q_codes = sb.tile([P, Q], U32, align_bytes=64)
+        q_plane = sb.tile([P, Q], U8, align_bytes=64)
+        nc.vector.quantize_mx(
+            out=q_codes[:].bitcast(FP8X4), scales=q_plane[:], in_=q_grouped[:].rearrange("p w j -> p (w j)")
+        )
+
+        b = sb.tile([P, U], F32)
+        NB = 256
+        for c in range(U // NB):
+            bank = psum.tile([P, NB], F32, name="bank_b%d" % c)
+            cols = slice(c * NB, (c + 1) * NB)
+            nc.tensor.matmul_mx(
+                out=bank[:],
+                lhsT=q_codes[:].bitcast(FP8X4),
+                lhsT_scale=q_plane[:],
+                rhs=notes_codes[:, 2 * c * NB : 2 * (c + 1) * NB].bitcast(FP4X4),
+                rhs_scale=notes_plane[:, cols],
+                start=True,
+                stop=True,
+            )
+            if c % 2 == 0:
+                nc.scalar.activation(b[:, cols], bank[:], COPY)
+            else:
+                nc.vector.tensor_copy(b[:, cols], bank[:])
+
+        b2 = sb.tile([P, I], F32)
+        nc.vector.tensor_copy(b2[:, :HALF], b[:].indirect(half(list2, 0)))
+        nc.scalar.activation(b2[:, HALF:], b[:].indirect(half(list2, 1)), COPY)
+        nc.vector.tensor_copy(f2[:].indirect(list4[:]), b2[:])
+
+        a = sb.tile([P, T], F32)
+        NA = 512
+        for c in range(T // NA):
+            bank = psum.tile([P, NA], F32, name="bank_a%d" % c)
+            cols = slice(c * NA, (c + 1) * NA)
+            nc.tensor.matmul_mx(
+                out=bank[:],
+                lhsT=q_codes[:].bitcast(FP8X4),
+                lhsT_scale=q_plane[:],
+                rhs=keys_codes[:, cols].bitcast(FP8X4),
+                rhs_scale=keys_plane[:, cols],
+                start=True,
+                stop=True,
+            )
+            nc.scalar.activation(a[:, cols], bank[:], COPY)
+
+        a1 = sb.tile([P, I], F32)
+        nc.scalar.activation(a1[:], a[:].indirect(list1[:]), COPY)
+        nc.vector.tensor_copy(f1[:].indirect(list3[:]), a1[:])
+
+        b5 = sb.tile([P, I], F32)
+        nc.scalar.activation(b5[:], b[:].indirect(list5[:]), COPY)
+        a6 = sb.tile([P, I], F32)
+        nc.scalar.activation(a6[:], a[:].indirect(list6[:]), COPY)
+
+        m1 = sb.tile([P, Z], F32)
+        nc.vector.tensor_tensor(m1[:], f1[:], f2[:], ALU.min)
+
+        g = [sb.tile([P, HALF], F32, name="g%d" % h) for h in range(2)]
+        m4 = [sb.tile([P, HALF], F32, name="m4_%d" % h) for h in range(2)]
+        v = [sb.tile([P, HALF], F32, name="v%d" % h) for h in range(2)]
+        y = [sb.tile([P, HALF], F32, name="y%d" % h) for h in range(2)]
+        cols = [slice(h * HALF, (h + 1) * HALF) for h in range(2)]
+        for h in range(2):
+            nc.vector.tensor_tensor(g[h][:], m1[:].indirect(half(list3, h)), b5[:, cols[h]], ALU.subtract)
+            nc.scalar.activation(m4[h][:], m1[:].indirect(half(list4, h)), COPY)
+        for h in range(2):
+            nc.vector.tensor_tensor(v[h][:], g[h][:], m4[h][:], ALU.add)
+        for h in range(2):
+            nc.vector.tensor_tensor(y[h][:], v[h][:], a6[:, cols[h]], ALU.max)
+            queue = nc.sync if h == 0 else nc.scalar
+            queue.dma_start(out[:, cols[h]], y[h][:])

@@ -55,12 +55,12 @@ def tile_attend_foldedback_two_kernel(
         nc.sync.dma_start(q_raw[:], query.rearrange("(p j) w -> p j w", j=PACK))
         notes_codes = sb.tile([P, 2 * U], U8, align_bytes=64)
         nc.sync.dma_start(notes_codes[:].bitcast(I32), notes_words[0].bitcast(I32))
-        load_plane(nc.sync, notes_plane, notes_scales)
         list2 = load_list(offs2, "list2")
-        list4 = load_list(offs4, "list4")
+        load_plane(nc.sync, notes_plane, notes_scales)
         keys_codes = sb.tile([P, T], U32, align_bytes=64)
         nc.sync.dma_start(keys_codes[:].bitcast(I32), keys_words[0].rearrange("p n t -> p (n t)").bitcast(I32))
         load_plane(nc.sync, keys_plane, keys_scales)
+        list4 = load_list(offs4, "list4")
         list1 = load_list(offs, "list1")
         list3 = load_list(offs3, "list3")
         list5 = load_list(offs5, "list5")
@@ -69,34 +69,40 @@ def tile_attend_foldedback_two_kernel(
         f1 = sb.tile([P, Z], F32)
         f2 = sb.tile([P, Z], F32)
         nc.vector.memset(f2[:], 0.0)
-        nc.gpsimd.memset(f1[:], 0.0)
+        nc.vector.memset(f1[:], 0.0)
 
         q_grouped = sb.tile([P, Q, PACK], BF16, align_bytes=64)
-        nc.vector.tensor_copy(q_grouped[:], q_raw[:].rearrange("p j w -> p w j"))
         q_codes = sb.tile([P, Q], U32, align_bytes=64)
         q_plane = sb.tile([P, Q], U8, align_bytes=64)
-        nc.vector.quantize_mx(
-            out=q_codes[:].bitcast(FP8X4), scales=q_plane[:], in_=q_grouped[:].rearrange("p w j -> p (w j)")
-        )
+        q_halves = [slice(0, Q // 2), slice(Q // 2, Q)]
+        for cols in q_halves:
+            nc.vector.tensor_copy(q_grouped[:, cols, :], q_raw[:, :, cols].rearrange("p j w -> p w j"))
+        for cols in q_halves:
+            nc.vector.quantize_mx(
+                out=q_codes[:, cols].bitcast(FP8X4),
+                scales=q_plane[:, cols],
+                in_=q_grouped[:, cols, :].rearrange("p w j -> p (w j)"),
+            )
 
         b = sb.tile([P, U], F32)
-        NB = 256
-        for c in range(U // NB):
-            bank = psum.tile([P, NB], F32, name="bank_b%d" % c)
-            cols = slice(c * NB, (c + 1) * NB)
+        start = 0
+        for c, width in enumerate((256, 256, 256, 128, 128)):
+            bank = psum.tile([P, width], F32, name="bank_b%d" % c)
+            cols = slice(start, start + width)
             nc.tensor.matmul_mx(
                 out=bank[:],
                 lhsT=q_codes[:].bitcast(FP8X4),
                 lhsT_scale=q_plane[:],
-                rhs=notes_codes[:, 2 * c * NB : 2 * (c + 1) * NB].bitcast(FP4X4),
+                rhs=notes_codes[:, 2 * start : 2 * (start + width)].bitcast(FP4X4),
                 rhs_scale=notes_plane[:, cols],
                 start=True,
                 stop=True,
             )
+            start += width
             if c % 2 == 0:
-                nc.scalar.activation(b[:, cols], bank[:], COPY)
-            else:
                 nc.vector.tensor_copy(b[:, cols], bank[:])
+            else:
+                nc.scalar.activation(b[:, cols], bank[:], COPY)
 
         b2 = sb.tile([P, I], F32)
         nc.vector.tensor_copy(b2[:, :HALF], b[:].indirect(half(list2, 0)))

from contextlib import ExitStack

import concourse.mybir as mybir

D, T, U, Z, I, Q = 512, 1024, 1024, 1024, 512, 128
FLOPS = 2 * D * Q * (T + U)

F32 = mybir.dt.float32
BF16 = mybir.dt.bfloat16
I32 = mybir.dt.int32
U32 = mybir.dt.uint32
U16 = mybir.dt.uint16
U8 = mybir.dt.uint8
FP8X4 = mybir.dt.float8_e4m3fn_x4
FP4X4 = mybir.dt.float4_e2m1fn_x4
ALU = mybir.AluOpType
COPY = mybir.ActivationFunctionType.Copy

P = 128
PACK = 4
HALF = I // 2
LIST_COLS = I // 16


def tile_attend_foldedback_two_kernel(
    tc, query, keys_words, keys_scales, notes_words, notes_scales, offs, offs2, offs3, offs4, offs5, offs6, out
):
    nc = tc.nc
    with ExitStack() as ctx:
        lists = ctx.enter_context(tc.tile_pool(name="lists", bufs=1))
        sb = ctx.enter_context(tc.tile_pool(name="sb", bufs=1))
        psum = ctx.enter_context(tc.psum_pool(name="psum", bufs=1))

        def load_list(src, name):
            t = lists.tile([P, LIST_COLS], U16, name=name)
            nc.sync.dma_start(t[:], src)
            return t

        def load_plane(queue, plane, scales):
            for quad in range(4):
                queue.dma_start(
                    plane[32 * quad : 32 * quad + 4, :].bitcast(I32),
                    scales[0, 4 * quad : 4 * quad + 4, :].bitcast(I32),
                )

        def half(t, h):
            return t[:, h * (LIST_COLS // 2) : (h + 1) * (LIST_COLS // 2)]

        notes_plane = sb.tile([P, U], U8, align_bytes=64)
        keys_plane = sb.tile([P, T], U8, align_bytes=64)
        nc.vector.memset(notes_plane[:].bitcast(I32), 0)
        nc.vector.memset(keys_plane[:].bitcast(I32), 0)

        q_raw = sb.tile([P, PACK, Q], F32)
        nc.sync.dma_start(q_raw[:], query.rearrange("(p j) w -> p j w", j=PACK))
        notes_codes = sb.tile([P, 2 * U], U8, align_bytes=64)
        nc.sync.dma_start(notes_codes[:].bitcast(I32), notes_words[0].bitcast(I32))
        list2 = load_list(offs2, "list2")
        load_plane(nc.sync, notes_plane, notes_scales)
        keys_codes = sb.tile([P, T], U32, align_bytes=64)
        nc.sync.dma_start(keys_codes[:].bitcast(I32), keys_words[0].rearrange("p n t -> p (n t)").bitcast(I32))
        load_plane(nc.sync, keys_plane, keys_scales)
        list4 = load_list(offs4, "list4")
        list1 = load_list(offs, "list1")
        list3 = load_list(offs3, "list3")
        list5 = load_list(offs5, "list5")
        list6 = load_list(offs6, "list6")

        f1 = sb.tile([P, Z], F32)
        f2 = sb.tile([P, Z], F32)
        nc.vector.memset(f2[:], 0.0)
        nc.vector.memset(f1[:], 0.0)

        q_grouped = sb.tile([P, Q, PACK], BF16, align_bytes=64)
        q_codes = sb.tile([P, Q], U32, align_bytes=64)
        q_plane = sb.tile([P, Q], U8, align_bytes=64)
        q_halves = [slice(0, Q // 2), slice(Q // 2, Q)]
        for cols in q_halves:
            nc.vector.tensor_copy(q_grouped[:, cols, :], q_raw[:, :, cols].rearrange("p j w -> p w j"))
        for cols in q_halves:
            nc.vector.quantize_mx(
                out=q_codes[:, cols].bitcast(FP8X4),
                scales=q_plane[:, cols],
                in_=q_grouped[:, cols, :].rearrange("p w j -> p (w j)"),
            )

        b = sb.tile([P, U], F32)
        start = 0
        for c, width in enumerate((256, 256, 256, 128, 128)):
            bank = psum.tile([P, width], F32, name="bank_b%d" % c)
            cols = slice(start, start + width)
            nc.tensor.matmul_mx(
                out=bank[:],
                lhsT=q_codes[:].bitcast(FP8X4),
                lhsT_scale=q_plane[:],
                rhs=notes_codes[:, 2 * start : 2 * (start + width)].bitcast(FP4X4),
                rhs_scale=notes_plane[:, cols],
                start=True,
                stop=True,
            )
            start += width
            if c % 2 == 0:
                nc.vector.tensor_copy(b[:, cols], bank[:])
            else:
                nc.scalar.activation(b[:, cols], bank[:], COPY)

        b2 = sb.tile([P, I], F32)
        nc.vector.tensor_copy(b2[:, :HALF], b[:].indirect(half(list2, 0)))
        nc.scalar.activation(b2[:, HALF:], b[:].indirect(half(list2, 1)), COPY)
        nc.vector.tensor_copy(f2[:].indirect(list4[:]), b2[:])

        a = sb.tile([P, T], F32)
        NA = 512
        for c in range(T // NA):
            bank = psum.tile([P, NA], F32, name="bank_a%d" % c)
            cols = slice(c * NA, (c + 1) * NA)
            nc.tensor.matmul_mx(
                out=bank[:],
                lhsT=q_codes[:].bitcast(FP8X4),
                lhsT_scale=q_plane[:],
                rhs=keys_codes[:, cols].bitcast(FP8X4),
                rhs_scale=keys_plane[:, cols],
                start=True,
                stop=True,
            )
            nc.scalar.activation(a[:, cols], bank[:], COPY)

        a1 = sb.tile([P, I], F32)
        nc.scalar.activation(a1[:], a[:].indirect(list1[:]), COPY)
        nc.vector.tensor_copy(f1[:].indirect(list3[:]), a1[:])

        b5 = sb.tile([P, I], F32)
        nc.scalar.activation(b5[:], b[:].indirect(list5[:]), COPY)
        a6 = sb.tile([P, I], F32)
        nc.scalar.activation(a6[:], a[:].indirect(list6[:]), COPY)

        m1 = sb.tile([P, Z], F32)
        nc.vector.tensor_tensor(m1[:], f1[:], f2[:], ALU.min)

        g = [sb.tile([P, HALF], F32, name="g%d" % h) for h in range(2)]
        m4 = [sb.tile([P, HALF], F32, name="m4_%d" % h) for h in range(2)]
        v = [sb.tile([P, HALF], F32, name="v%d" % h) for h in range(2)]
        y = [sb.tile([P, HALF], F32, name="y%d" % h) for h in range(2)]
        cols = [slice(h * HALF, (h + 1) * HALF) for h in range(2)]
        for h in range(2):
            nc.vector.tensor_tensor(g[h][:], m1[:].indirect(half(list3, h)), b5[:, cols[h]], ALU.subtract)
            nc.scalar.activation(m4[h][:], m1[:].indirect(half(list4, h)), COPY)
        for h in range(2):
            nc.vector.tensor_tensor(v[h][:], g[h][:], m4[h][:], ALU.add)
        for h in range(2):
            nc.vector.tensor_tensor(y[h][:], v[h][:], a6[:, cols[h]], ALU.max)
            queue = nc.sync if h == 0 else nc.scalar
            queue.dma_start(out[:, cols[h]], y[h][:])
